import numpy as np
import ml_dtypes


def mxq(x, axis, fmt="e4m3"):
    dtype, down = {"e4m3": (ml_dtypes.float8_e4m3fn, 7), "e5m2": (ml_dtypes.float8_e5m2, 14)}[fmt]
    v = np.moveaxis(np.asarray(x, np.float32).astype(ml_dtypes.bfloat16).astype(np.float64), axis, -1)
    blocks = v.reshape(v.shape[:-1] + (-1, 32))
    amax = np.abs(blocks).max(-1, keepdims=True)
    byte = np.maximum(np.where(amax > 0, np.frexp(amax)[1] - 1 + 127, 0) - down, 1)
    scale = np.exp2(byte - 127.0)
    codes = (blocks / scale).astype(np.float32).astype(dtype).astype(np.float64)
    return np.moveaxis((codes * scale).reshape(v.shape), -1, axis)


WIDE = False


def mx_kscale(k):
    if not WIDE:
        return np.ones(k)
    levels = np.array([10, -10, 5, -5, 0])
    if k % 512:
        return np.exp2(np.random.permutation(np.resize(levels, k // 32))).repeat(32)
    a = np.empty((k // 512, 16))
    for p in range(k // 512):
        a[p, :8] = np.random.permutation(np.resize(levels, 8))
        for g in range(8):
            far = levels[np.abs(levels - a[p, g]) >= 10]
            a[p, g + 8] = far[np.random.randint(len(far))]
    return np.exp2(a.ravel()).repeat(32)


def f64(x):
    return np.asarray(x).astype(np.float64)


def striped(idx):
    return np.tile(idx.reshape(-1, 16).T, (8, 1)).astype(np.uint16)


def unstriped(offs):
    return offs[:16].T.reshape(-1).astype(np.int64)


E2M1 = np.array([0.0, 0.5, 1.0, 1.5, 2.0, 3.0, 4.0, 6.0, -0.0, -0.5, -1.0, -1.5, -2.0, -3.0, -4.0, -6.0])


def pack_weight(w, fmt):
    k, n = w.shape
    w = f64(np.asarray(w, np.float32).astype(ml_dtypes.bfloat16)).reshape(k // 32, 32, n)
    amax = np.abs(w).max(1)
    if fmt == "e4m3":
        byte = np.frexp(amax)[1] - 1 + 127 - 7
    else:
        mant, ex = np.frexp(amax / 6.0)
        byte = np.where(mant > 0.5, ex, ex - 1) + 127
    byte = np.clip(np.where(amax > 0, byte, 1), 1, 254)
    scaled = (w * np.exp2(127.0 - byte)[:, None, :]).reshape(k, n).astype(np.float32)
    by_word = np.ascontiguousarray(scaled.reshape(k // 512, 128, 4, n).transpose(0, 1, 3, 2))
    if fmt == "e4m3":
        words = by_word.astype(ml_dtypes.float8_e4m3fn).view(np.uint8)
    else:
        c = by_word.astype(ml_dtypes.float4_e2m1fn).view(np.uint8) & 0xF
        words = (c[..., 0::2] | (c[..., 1::2] << 4)).reshape(k // 512, 128, 2 * n)
    return np.ascontiguousarray(words), np.ascontiguousarray(byte.astype(np.uint8).reshape(k // 512, 16, n))


def unpack_weight(words, scales, fmt):
    g, _, n = scales.shape
    words = np.ascontiguousarray(words).reshape(g, 128, n, -1)
    if fmt == "e4m3":
        vals = words.view(ml_dtypes.float8_e4m3fn).astype(np.float64)
    else:
        nib = np.empty((g, 128, n, 4), np.uint8)
        nib[..., 0::2] = words & 0xF
        nib[..., 1::2] = words >> 4
        vals = E2M1[nib]
    vals = vals * np.repeat(np.exp2(scales.astype(np.float64) - 127.0), 8, axis=1)[..., None]
    return vals.transpose(0, 1, 3, 2).reshape(g * 512, n)


def gelu(v):
    return 0.5 * v * (1.0 + np.tanh(np.sqrt(2.0 / np.pi) * (v + 0.044715 * v**3)))


def often(T, S):
    return np.random.permutation(T)[(T * np.random.uniform(0, 1, S) ** 4).astype(np.int64)]


K, K2, H, N, T, S, P = 1024, 512, 1024, 512, 4096, 1024, 512


def setup_inputs():
    n = np.random.standard_normal
    s = mx_kscale(K)[:, None]
    s2 = mx_kscale(K2)[:, None]
    u = mx_kscale(H)[:, None]
    d = {}
    d["tab_words"], d["tab_scales"] = pack_weight(n((K, T)) * s, "e4m3")
    d["tab2_words"], d["tab2_scales"] = pack_weight(n((K2, T)) * s2, "e4m3")
    d["tab3_words"], d["tab3_scales"] = pack_weight(n((K2, T)) * s2, "e4m3")
    d["offs"] = striped(np.random.permutation(T)[:S])
    d["offs2"] = striped(np.random.permutation(T)[:S])
    d["offs3"] = striped(np.random.permutation(T)[:S])
    d["pos1"] = striped(np.random.permutation(S)[:P])
    d["pos2"] = striped(often(S, P))
    d["pos3"] = striped(often(S, P))
    d["w1"] = (n((K, H)) / K ** 0.5 / s).astype(np.float32)
    d["w2_words"], d["w2_scales"] = pack_weight(n((K2, H)) / K2 ** 0.5 / s2, "e4m3")
    d["w3"] = (n((K2, H)) / K2 ** 0.5 / s2 * u.T).astype(np.float32)
    d["bd"] = (0.5 * n(H) * u[:, 0]).astype(np.float32)
    d["w4_words"], d["w4_scales"] = pack_weight(n((H, N)) / H ** 0.5 / u, "e2m1")
    d["w5"] = (n((H, N)) / H ** 0.5 / u).astype(np.float32)
    d["bo"] = (0.5 * n(N)).astype(np.float32)
    return d


def reference(tab_words, tab_scales, tab2_words, tab2_scales, tab3_words, tab3_scales, offs, offs2, offs3, pos1, pos2, pos3, w1, w2_words, w2_scales, w3, bd, w4_words, w4_scales, w5, bo):
    v = unpack_weight(tab_words, tab_scales, "e4m3")[:, unstriped(offs)]
    v2 = unpack_weight(tab2_words, tab2_scales, "e4m3")[:, unstriped(offs2)]
    v3 = unpack_weight(tab3_words, tab3_scales, "e4m3")[:, unstriped(offs3)]
    a = mxq(f64(w1), 0, "e4m3").T @ v
    b = unpack_weight(w2_words, w2_scales, "e4m3").T @ v2
    d = (mxq(f64(w3), 0, "e4m3").T @ v3) + f64(bd)[:, None]
    ap = a[:, unstriped(pos1)]
    bp = b[:, unstriped(pos2)]
    dp = d[:, unstriped(pos3)]
    z = (ap - bp) / (1.0 + np.abs(bp)) * dp
    y = unpack_weight(w4_words, w4_scales, "e2m1").T @ mxq(z, 0, "e4m3") + mxq(f64(w5), 0, "e4m3").T @ mxq(dp, 0, "e4m3")
    return y + f64(bo)[:, None]

@@ -1,0 +1,264 @@
+from contextlib import ExitStack
+
+import concourse.mybir as mybir
+
+K, K2, H, N, T, S, PICKS = 1024, 512, 1024, 512, 4096, 1024, 512
+FLOPS = 2 * (K * H * S + 2 * K2 * H * S + 2 * H * N * PICKS)
+
+F32 = mybir.dt.float32
+BF16 = mybir.dt.bfloat16
+I32 = mybir.dt.int32
+U32 = mybir.dt.uint32
+U16 = mybir.dt.uint16
+U8 = mybir.dt.uint8
+FP8X4 = mybir.dt.float8_e4m3fn_x4
+FP4X4 = mybir.dt.float4_e2m1fn_x4
+ALU = mybir.AluOpType
+ACT = mybir.ActivationFunctionType
+
+P = 128
+PACK = 4
+PASS = P * PACK
+BANK = 512
+QUADS = 4
+
+
+def tile_list_shade_finder_contrast_kernel(
+    tc, tab_words, tab_scales, tab2_words, tab2_scales, tab3_words, tab3_scales,
+    offs, offs2, offs3, pos1, pos2, pos3,
+    w1, w2_words, w2_scales, w3, bd, w4_words, w4_scales, w5, bo, out,
+):
+    nc = tc.nc
+    with ExitStack() as ctx:
+        lists = ctx.enter_context(tc.tile_pool(name="lists", bufs=1))
+        keep = ctx.enter_context(tc.tile_pool(name="keep", bufs=1))
+        tables = ctx.enter_context(tc.tile_pool(name="tables", bufs=1))
+        raws = ctx.enter_context(tc.tile_pool(name="raws", bufs=1))
+        rounded = ctx.enter_context(tc.tile_pool(name="rounded", bufs=1))
+        rows = ctx.enter_context(tc.tile_pool(name="rows", bufs=1))
+        results = ctx.enter_context(tc.tile_pool(name="results", bufs=4))
+        psum = ctx.enter_context(tc.psum_pool(name="psum", bufs=4))
+
+        used = {"raw": 0, "rounded": 0, "rows": 0}
+
+        def next_tag(kind, slots):
+            used[kind] = used[kind] + 1
+            return "%s%d" % (kind, (used[kind] - 1) % slots)
+
+        def load_list(name, dram):
+            tile = lists.tile(list(dram.shape), U16, name=name)
+            nc.sync.dma_start(tile[:], dram)
+            return tile
+
+        def zeroed_bytes(name, shape):
+            tile = keep.tile(shape, U8, name=name, align_bytes=64)
+            nc.vector.memset(tile[:].bitcast(I32), 0)
+            return tile
+
+        def load_scale_rows(tile, dram, first):
+            passes = dram.shape[0]
+            for q in range(QUADS):
+                lo = 32 * q + first
+                src = dram[:, 4 * q : 4 * q + 4, :] if passes > 1 else dram[0, 4 * q : 4 * q + 4, :]
+                nc.sync.dma_start(tile[lo : lo + 4 * passes, :].bitcast(I32), src.bitcast(I32))
+
+        def load_table(name, dram, slot):
+            tile = tables.tile([P, T], I32, name=name, tag="table%d" % slot, align_bytes=64)
+            nc.sync.dma_start(tile[:], dram.rearrange("p t i -> p (t i)").bitcast(I32))
+            return tile
+
+        def load_raw(name, dram):
+            tile = raws.tile([P, PACK, BANK], F32, name=name, tag=next_tag("raw", 3))
+            nc.sync.dma_start(tile[:], dram.rearrange("(p j) c -> p j c", j=PACK))
+            return tile
+
+        def gather_words(name, table, offsets):
+            tile = keep.tile([P, S], U32, name=name, align_bytes=64)
+            nc.vector.tensor_copy(tile[:], table[:].bitcast(U32).indirect(offsets[:]))
+            return tile
+
+        def gather_bytes(name, plane, offsets):
+            tile = keep.tile([P, S], U8, name=name, align_bytes=64)
+            nc.vector.tensor_copy(tile[:], plane[:].indirect(offsets[:]))
+            return tile
+
+        def new_rounded(name):
+            return rounded.tile([P, PACK * BANK], BF16, name=name, tag=next_tag("rounded", 4), align_bytes=64)
+
+        def dealt_views(dst, raw, lo, hi):
+            o = dst[:].rearrange("p (t m j) -> p m j t", t=PACK, j=PACK)[:, lo:hi]
+            i = raw[:].rearrange("p j (m t) -> p m j t", t=PACK)[:, lo:hi]
+            return o, i
+
+        def woven_out(dst):
+            return dst[:].rearrange("p (c i j) -> p c j i", i=4, j=PACK)
+
+        def woven_in(src):
+            return src.rearrange("p j (c i) -> p c j i", i=4)
+
+        def round_dealt(dst, raw):
+            for t in range(PACK):
+                o = dst[:].rearrange("p (t m j) -> p t m j", t=PACK, j=PACK)[:, t]
+                i = raw[:].rearrange("p j (m t) -> p t m j", t=PACK)[:, t]
+                nc.gpsimd.tensor_scalar(o, i, 1.0, 0.0, ALU.mult, ALU.add)
+            return dst
+
+        def quantize(name, src):
+            codes = keep.tile([P, BANK], U32, name=name + "_codes", align_bytes=64)
+            scales = keep.tile([P, BANK], U8, name=name + "_scales", align_bytes=64)
+            nc.vector.quantize_mx(out=codes[:].bitcast(FP8X4), scales=scales[:], in_=src[:])
+            return codes, scales
+
+        def first_stage(name, passes, t, bias):
+            cols = slice(P * t, P * t + P)
+            window = rows.tile([P, S], F32, name=name, tag=next_tag("rows", 6))
+            for h in range(S // BANK):
+                half = slice(BANK * h, BANK * h + BANK)
+                acc = psum.tile([P, BANK], F32, name=name + "_acc", tag="acc")
+                for a, (codes, scales, words, plane, first) in enumerate(passes):
+                    nc.tensor.matmul_mx(
+                        out=acc[:], lhsT=codes[:, cols].bitcast(FP8X4), lhsT_scale=scales[:, cols],
+                        rhs=words[:, half].bitcast(FP8X4), rhs_scale=plane[first:P, half],
+                        start=(a == 0), stop=(a == len(passes) - 1),
+                    )
+                if bias is None:
+                    nc.scalar.copy(window[:, half], acc[:])
+                else:
+                    nc.scalar.activation(window[:, half], acc[:], ACT.Identity, bias=bias)
+            return window
+
+        def round_woven(dst, raw):
+            for h in range(4):
+                o = dst[:].rearrange("p (c j) -> p c j", j=PACK)[:, P * h : P * h + P]
+                i = raw[:].rearrange("p j c -> p c j")[:, P * h : P * h + P]
+                nc.gpsimd.tensor_scalar(o, i, 1.0, 0.0, ALU.mult, ALU.add)
+            return dst
+
+        def w1_block(g, a):
+            return load_raw("w1_raw", w1[PASS * a : PASS * a + PASS, BANK * g : BANK * g + BANK])
+
+        tab2_plane = zeroed_bytes("tab2_plane", [P, T])
+        w2_plane = zeroed_bytes("w2_plane", [P, H])
+        tab3_plane = zeroed_bytes("tab3_plane", [P, T])
+        tab_plane = zeroed_bytes("tab_plane", [P, T])
+        w4_plane = zeroed_bytes("w4_plane", [P, 2 * N])
+
+        offs2_sb = load_list("offs2_sb", offs2)
+        load_scale_rows(tab2_plane, tab2_scales, 8)
+        tab2_sb = load_table("tab2_sb", tab2_words[0], 0)
+        w2_sb = keep.tile([P, H], I32, name="w2_sb", align_bytes=64)
+        nc.sync.dma_start(w2_sb[:], w2_words[0].rearrange("p c i -> p (c i)").bitcast(I32))
+        load_scale_rows(w2_plane, w2_scales, 0)
+        offs3_sb = load_list("offs3_sb", offs3)
+        load_scale_rows(tab3_plane, tab3_scales, 12)
+        tab3_sb = load_table("tab3_sb", tab3_words[0], 1)
+        pos2_sb = load_list("pos2_sb", pos2)
+        offs_sb = load_list("offs_sb", offs)
+        load_scale_rows(tab_plane, tab_scales, 0)
+        bd_sb = lists.tile([P, 2, PACK], F32, name="bd_sb")
+        nc.sync.dma_start(bd_sb[:], bd.rearrange("(g p t) -> p g t", p=P, t=PACK))
+        w3_raw = [load_raw("w3_raw", w3[:, BANK * g : BANK * g + BANK]) for g in range(2)]
+        pos3_sb = load_list("pos3_sb", pos3)
+
+        v2_scales = gather_bytes("v2_scales", tab2_plane, offs2_sb)
+        v2_words = gather_words("v2_words", tab2_sb, offs2_sb)
+        w2_codes = keep.tile([P, H], I32, name="w2_codes", align_bytes=64)
+        nc.vector.tensor_copy(
+            w2_codes[:].rearrange("p (g t m) -> p g m t", g=2, t=PACK),
+            w2_sb[:].rearrange("p (g m t) -> p g m t", g=2, t=PACK),
+        )
+        w2_dealt = keep.tile([P, H], U8, name="w2_dealt", align_bytes=64)
+        nc.vector.tensor_copy(
+            w2_dealt[:].rearrange("p (g t m) -> p g t m", g=2, t=PACK),
+            w2_plane[:].rearrange("p (g m t) -> p g t m", g=2, t=PACK),
+        )
+        v3_scales = gather_bytes("v3_scales", tab3_plane, offs3_sb)
+        v3_words = gather_words("v3_words", tab3_sb, offs3_sb)
+        v_scales = gather_bytes("v_scales", tab_plane, offs_sb)
+
+        bp = []
+        w3_q = []
+        for g in range(2):
+            gc = slice(BANK * g, BANK * g + BANK)
+            bp.append(keep.tile([P, PACK, PICKS], F32, name="bp%d" % g, tag="bp%d" % g, align_bytes=64))
+            for t in range(PACK):
+                window = first_stage("b_rows", [(w2_codes[:, gc], w2_dealt[:, gc], v2_words, v2_scales, 8)], t, None)
+                nc.vector.tensor_copy(bp[g][:, t, :], window[:].indirect(pos2_sb[:]))
+            if g == 0:
+                w3_bf = keep.tile([P, PACK * BANK], BF16, name="w3_bf", tag="bp1", align_bytes=64)
+            else:
+                w3_bf = new_rounded("w3_bf")
+            w3_q.append(quantize("w3_%d" % g, round_dealt(w3_bf, w3_raw[g])))
+
+        w1_raw = [w1_block(0, a) for a in range(2)]
+        tab_sb = [load_table("tab_sb", tab_words[a], a) for a in range(2)]
+        w1_q = [quantize("w1_0%d" % a, round_dealt(new_rounded("w1_bf"), w1_raw[a])) for a in range(2)]
+        w1_raw = [w1_block(1, a) for a in range(2)]
+        pos1_sb = load_list("pos1_sb", pos1)
+
+        dp = []
+        v_words = []
+        fac = []
+        for g in range(2):
+            v_words.append(gather_words("v_words%d" % g, tab_sb[g], offs_sb))
+            codes, scales = w3_q[g]
+            dp.append(tables.tile([P, PACK, PICKS], F32, name="dp", tag="table%d" % g, align_bytes=64))
+            for t in range(PACK):
+                window = first_stage("d_rows", [(codes, scales, v3_words, v3_scales, 12)], t, bd_sb[:, g, t : t + 1])
+                nc.vector.tensor_copy(dp[g][:, t, :], window[:].indirect(pos3_sb[:]))
+            fac.append(keep.tile([P, PACK, PICKS], F32, name="fac%d" % g))
+            nc.scalar.activation(fac[g][:], bp[g][:], ACT.Abs)
+            nc.scalar.activation(fac[g][:], fac[g][:], ACT.Abs_reciprocal_sqrt, bias=1.0)
+            nc.scalar.activation(fac[g][:], fac[g][:], ACT.Square)
+
+        w1_q = w1_q + [quantize("w1_1%d" % a, round_dealt(new_rounded("w1_bf"), w1_raw[a])) for a in range(2)]
+        w5_raw = [load_raw("w5_raw", w5[PASS * g : PASS * g + PASS, :]) for g in range(2)]
+        w4_sb = keep.tile([P, 2, 2 * N], U8, name="w4_sb", align_bytes=64)
+        nc.sync.dma_start(w4_sb[:].bitcast(I32), w4_words.rearrange("a p n -> p a n").bitcast(I32))
+        for q in range(QUADS):
+            nc.sync.dma_start(
+                w4_plane[32 * q : 32 * q + 4, :].rearrange("r (a n) -> r a n", a=2).bitcast(I32),
+                w4_scales[:, 4 * q : 4 * q + 4, :].rearrange("a r n -> r a n").bitcast(I32),
+            )
+        bo_sb = lists.tile([P, N // P], F32, name="bo_sb")
+        with nc.allow_non_contiguous_dma(reason="one bias value a partition"):
+            nc.sync.dma_start(bo_sb[:], bo.rearrange("(c p) -> p c", p=P))
+        w5_q = [quantize("w5_%d" % g, round_woven(new_rounded("w5_bf"), w5_raw[g])) for g in range(2)]
+
+        final = [psum.tile([P, PICKS], F32, name="final%d" % c, tag="final") for c in range(N // P)]
+        diff = []
+        for g in range(2):
+            diff.append(keep.tile([P, PACK, PICKS], F32, name="diff%d" % g))
+            for t in range(PACK):
+                passes = [(w1_q[2 * g + a][0], w1_q[2 * g + a][1], v_words[a], v_scales, 4 * a) for a in range(2)]
+                window = first_stage("a_rows", passes, t, None)
+                nc.vector.tensor_tensor(diff[g][:, t, :], window[:].indirect(pos1_sb[:]), bp[g][:, t, :], ALU.subtract)
+        for g in range(2):
+            nc.vector.tensor_tensor(fac[g][:], fac[g][:], dp[g][:], ALU.mult)
+            dp_bf = new_rounded("dp_bf")
+            nc.scalar.copy(woven_out(dp_bf), woven_in(dp[g][:]))
+            dp_codes, dp_scales = quantize("dp_%d" % g, dp_bf)
+            w5_codes, w5_scales = w5_q[g]
+            for c in range(N // P):
+                cols = slice(P * c, P * c + P)
+                nc.tensor.matmul_mx(
+                    out=final[c][:], lhsT=w5_codes[:, cols].bitcast(FP8X4), lhsT_scale=w5_scales[:, cols],
+                    rhs=dp_codes[:].bitcast(FP8X4), rhs_scale=dp_scales[:], start=(g == 0), stop=False,
+                )
+        for g in range(2):
+            z_bf = new_rounded("z_bf")
+            nc.vector.tensor_tensor(woven_out(z_bf), woven_in(diff[g][:]), woven_in(fac[g][:]), ALU.mult)
+            z_codes, z_scales = quantize("z_%d" % g, z_bf)
+            for c in range(N // P):
+                nc.tensor.matmul_mx(
+                    out=final[c][:], lhsT=w4_sb[:, g, 2 * P * c : 2 * P * c + 2 * P].bitcast(FP4X4),
+                    lhsT_scale=w4_plane[:, N * g + P * c : N * g + P * c + P],
+                    rhs=z_codes[:].bitcast(FP8X4), rhs_scale=z_scales[:], start=False, stop=(g == 1),
+                )
+        for c in range(N // P):
+            result = results.tile([P, PICKS], F32, name="result")
+            if c % 2 == 0:
+                nc.scalar.activation(result[:], final[c][:], ACT.Identity, bias=bo_sb[:, c : c + 1])
+            else:
+                nc.vector.tensor_scalar(result[:], final[c][:], bo_sb[:, c : c + 1], None, ALU.add)
+            nc.sync.dma_start(out[P * c : P * c + P, :], result[:])

@@ -36,10 +36,9 @@ def tile_list_shade_finder_contrast_kernel(
         raws = ctx.enter_context(tc.tile_pool(name="raws", bufs=1))
         rounded = ctx.enter_context(tc.tile_pool(name="rounded", bufs=1))
         rows = ctx.enter_context(tc.tile_pool(name="rows", bufs=1))
-        results = ctx.enter_context(tc.tile_pool(name="results", bufs=4))
-        psum = ctx.enter_context(tc.psum_pool(name="psum", bufs=4))
+        psum = ctx.enter_context(tc.psum_pool(name="psum", bufs=1))
 
-        used = {"raw": 0, "rounded": 0, "rows": 0}
+        used = {"raw": 0, "rounded": 0, "rows": 0, "bank": 0}
 
         def next_tag(kind, slots):
             used[kind] = used[kind] + 1
@@ -67,8 +66,8 @@ def tile_list_shade_finder_contrast_kernel(
             nc.sync.dma_start(tile[:], dram.rearrange("p t i -> p (t i)").bitcast(I32))
             return tile
 
-        def load_raw(name, dram):
-            tile = raws.tile([P, PACK, BANK], F32, name=name, tag=next_tag("raw", 3))
+        def load_raw(name, dram, slot):
+            tile = raws.tile([P, PACK, BANK], F32, name=name, tag="raw" + slot)
             nc.sync.dma_start(tile[:], dram.rearrange("(p j) c -> p j c", j=PACK))
             return tile
 
@@ -82,13 +81,8 @@ def tile_list_shade_finder_contrast_kernel(
             nc.vector.tensor_copy(tile[:], plane[:].indirect(offsets[:]))
             return tile
 
-        def new_rounded(name):
-            return rounded.tile([P, PACK * BANK], BF16, name=name, tag=next_tag("rounded", 4), align_bytes=64)
-
-        def dealt_views(dst, raw, lo, hi):
-            o = dst[:].rearrange("p (t m j) -> p m j t", t=PACK, j=PACK)[:, lo:hi]
-            i = raw[:].rearrange("p j (m t) -> p m j t", t=PACK)[:, lo:hi]
-            return o, i
+        def new_rounded(name, slot):
+            return rounded.tile([P, PACK * BANK], BF16, name=name, tag="rounded%d" % slot, align_bytes=64)
 
         def woven_out(dst):
             return dst[:].rearrange("p (c i j) -> p c j i", i=4, j=PACK)
@@ -96,11 +90,22 @@ def tile_list_shade_finder_contrast_kernel(
         def woven_in(src):
             return src.rearrange("p j (c i) -> p c j i", i=4)
 
-        def round_dealt(dst, raw):
-            for t in range(PACK):
-                o = dst[:].rearrange("p (t m j) -> p t m j", t=PACK, j=PACK)[:, t]
-                i = raw[:].rearrange("p j (m t) -> p t m j", t=PACK)[:, t]
-                nc.gpsimd.tensor_scalar(o, i, 1.0, 0.0, ALU.mult, ALU.add)
+        def copy_on(engine, o, i):
+            if engine == "scalar":
+                nc.scalar.copy(o, i)
+            else:
+                nc.vector.tensor_copy(o, i)
+
+        def round_dealt(dst, raw, engine):
+            copy_on(
+                engine,
+                dst[:].rearrange("p (t m j) -> p m j t", t=PACK, j=PACK),
+                raw[:].rearrange("p j (m t) -> p m j t", t=PACK),
+            )
+            return dst
+
+        def round_woven(dst, src, engine):
+            copy_on(engine, woven_out(dst), woven_in(src))
             return dst
 
         def quantize(name, src):
@@ -111,10 +116,10 @@ def tile_list_shade_finder_contrast_kernel(
 
         def first_stage(name, passes, t, bias):
             cols = slice(P * t, P * t + P)
-            window = rows.tile([P, S], F32, name=name, tag=next_tag("rows", 6))
+            window = rows.tile([P, S], F32, name=name, tag=next_tag("rows", 12), align_bytes=64)
             for h in range(S // BANK):
                 half = slice(BANK * h, BANK * h + BANK)
-                acc = psum.tile([P, BANK], F32, name=name + "_acc", tag="acc")
+                acc = psum.tile([P, BANK], F32, name=name + "_acc", tag=next_tag("bank", 8))
                 for a, (codes, scales, words, plane, first) in enumerate(passes):
                     nc.tensor.matmul_mx(
                         out=acc[:], lhsT=codes[:, cols].bitcast(FP8X4), lhsT_scale=scales[:, cols],
@@ -127,15 +132,8 @@ def tile_list_shade_finder_contrast_kernel(
                     nc.scalar.activation(window[:, half], acc[:], ACT.Identity, bias=bias)
             return window
 
-        def round_woven(dst, raw):
-            for h in range(4):
-                o = dst[:].rearrange("p (c j) -> p c j", j=PACK)[:, P * h : P * h + P]
-                i = raw[:].rearrange("p j c -> p c j")[:, P * h : P * h + P]
-                nc.gpsimd.tensor_scalar(o, i, 1.0, 0.0, ALU.mult, ALU.add)
-            return dst
-
-        def w1_block(g, a):
-            return load_raw("w1_raw", w1[PASS * a : PASS * a + PASS, BANK * g : BANK * g + BANK])
+        def w1_block(g, a, slot):
+            return load_raw("w1_raw", w1[PASS * a : PASS * a + PASS, BANK * g : BANK * g + BANK], slot)
 
         tab2_plane = zeroed_bytes("tab2_plane", [P, T])
         w2_plane = zeroed_bytes("w2_plane", [P, H])
@@ -144,75 +142,97 @@ def tile_list_shade_finder_contrast_kernel(
         w4_plane = zeroed_bytes("w4_plane", [P, 2 * N])
 
         offs2_sb = load_list("offs2_sb", offs2)
-        load_scale_rows(tab2_plane, tab2_scales, 8)
-        tab2_sb = load_table("tab2_sb", tab2_words[0], 0)
         w2_sb = keep.tile([P, H], I32, name="w2_sb", align_bytes=64)
         nc.sync.dma_start(w2_sb[:], w2_words[0].rearrange("p c i -> p (c i)").bitcast(I32))
+        load_scale_rows(tab2_plane, tab2_scales, 8)
+        tab2_sb = load_table("tab2_sb", tab2_words[0], 0)
         load_scale_rows(w2_plane, w2_scales, 0)
         offs3_sb = load_list("offs3_sb", offs3)
         load_scale_rows(tab3_plane, tab3_scales, 12)
-        tab3_sb = load_table("tab3_sb", tab3_words[0], 1)
         pos2_sb = load_list("pos2_sb", pos2)
+        tab3_sb = load_table("tab3_sb", tab3_words[0], 1)
         offs_sb = load_list("offs_sb", offs)
         load_scale_rows(tab_plane, tab_scales, 0)
+        w3_raw = [load_raw("w3_raw", w3[:, BANK * g : BANK * g + BANK], "AB"[g]) for g in range(2)]
         bd_sb = lists.tile([P, 2, PACK], F32, name="bd_sb")
         nc.sync.dma_start(bd_sb[:], bd.rearrange("(g p t) -> p g t", p=P, t=PACK))
-        w3_raw = [load_raw("w3_raw", w3[:, BANK * g : BANK * g + BANK]) for g in range(2)]
         pos3_sb = load_list("pos3_sb", pos3)
 
         v2_scales = gather_bytes("v2_scales", tab2_plane, offs2_sb)
-        v2_words = gather_words("v2_words", tab2_sb, offs2_sb)
         w2_codes = keep.tile([P, H], I32, name="w2_codes", align_bytes=64)
         nc.vector.tensor_copy(
             w2_codes[:].rearrange("p (g t m) -> p g m t", g=2, t=PACK),
             w2_sb[:].rearrange("p (g m t) -> p g m t", g=2, t=PACK),
         )
+        v2_words = gather_words("v2_words", tab2_sb, offs2_sb)
         w2_dealt = keep.tile([P, H], U8, name="w2_dealt", align_bytes=64)
         nc.vector.tensor_copy(
             w2_dealt[:].rearrange("p (g t m) -> p g t m", g=2, t=PACK),
             w2_plane[:].rearrange("p (g m t) -> p g t m", g=2, t=PACK),
         )
         v3_scales = gather_bytes("v3_scales", tab3_plane, offs3_sb)
-        v3_words = gather_words("v3_words", tab3_sb, offs3_sb)
-        v_scales = gather_bytes("v_scales", tab_plane, offs_sb)
 
-        bp = []
-        w3_q = []
-        for g in range(2):
+        def pick_b(g):
             gc = slice(BANK * g, BANK * g + BANK)
-            bp.append(keep.tile([P, PACK, PICKS], F32, name="bp%d" % g, tag="bp%d" % g, align_bytes=64))
+            tile = keep.tile([P, PACK, PICKS], F32, name="bp%d" % g, tag="bp%d" % g, align_bytes=64)
             for t in range(PACK):
                 window = first_stage("b_rows", [(w2_codes[:, gc], w2_dealt[:, gc], v2_words, v2_scales, 8)], t, None)
-                nc.vector.tensor_copy(bp[g][:, t, :], window[:].indirect(pos2_sb[:]))
-            if g == 0:
-                w3_bf = keep.tile([P, PACK * BANK], BF16, name="w3_bf", tag="bp1", align_bytes=64)
-            else:
-                w3_bf = new_rounded("w3_bf")
-            w3_q.append(quantize("w3_%d" % g, round_dealt(w3_bf, w3_raw[g])))
+                nc.vector.tensor_copy(tile[:, t, :], window[:].indirect(pos2_sb[:]))
+            return tile
 
-        w1_raw = [w1_block(0, a) for a in range(2)]
-        tab_sb = [load_table("tab_sb", tab_words[a], a) for a in range(2)]
-        w1_q = [quantize("w1_0%d" % a, round_dealt(new_rounded("w1_bf"), w1_raw[a])) for a in range(2)]
-        w1_raw = [w1_block(1, a) for a in range(2)]
-        pos1_sb = load_list("pos1_sb", pos1)
+        def damping(g):
+            tile = raws.tile([P, PACK, PICKS], F32, name="fac%d" % g, tag="raw" + "DB"[g])
+            nc.scalar.activation(tile[:], bp[g][:], ACT.Abs)
+            nc.scalar.activation(tile[:], tile[:], ACT.Abs_reciprocal_sqrt, bias=1.0)
+            nc.scalar.activation(tile[:], tile[:], ACT.Square)
+            return tile
 
-        dp = []
-        v_words = []
-        fac = []
-        for g in range(2):
-            v_words.append(gather_words("v_words%d" % g, tab_sb[g], offs_sb))
+        def damped_lamp(g):
+            damp = damping(g)
+            tile = raws.tile([P, PACK, PICKS], F32, name="wt%d" % g, tag="raw" + "AE"[g])
+            nc.vector.tensor_tensor(tile[:], damp[:], pair[g][:, 0], ALU.mult)
+            return tile
+
+        def pick_d(g, dst):
             codes, scales = w3_q[g]
-            dp.append(tables.tile([P, PACK, PICKS], F32, name="dp", tag="table%d" % g, align_bytes=64))
             for t in range(PACK):
                 window = first_stage("d_rows", [(codes, scales, v3_words, v3_scales, 12)], t, bd_sb[:, g, t : t + 1])
-                nc.vector.tensor_copy(dp[g][:, t, :], window[:].indirect(pos3_sb[:]))
-            fac.append(keep.tile([P, PACK, PICKS], F32, name="fac%d" % g))
-            nc.scalar.activation(fac[g][:], bp[g][:], ACT.Abs)
-            nc.scalar.activation(fac[g][:], fac[g][:], ACT.Abs_reciprocal_sqrt, bias=1.0)
-            nc.scalar.activation(fac[g][:], fac[g][:], ACT.Square)
+                nc.vector.tensor_copy(dst[:, t, :], window[:].indirect(pos3_sb[:]))
 
-        w1_q = w1_q + [quantize("w1_1%d" % a, round_dealt(new_rounded("w1_bf"), w1_raw[a])) for a in range(2)]
-        w5_raw = [load_raw("w5_raw", w5[PASS * g : PASS * g + PASS, :]) for g in range(2)]
+        def pick_a(g, dst):
+            passes = [(w1_q[g, a][0], w1_q[g, a][1], v_words[a], v_scales, 4 * a) for a in range(2)]
+            for t in range(PACK):
+                window = first_stage("a_rows", passes, t, None)
+                nc.vector.tensor_tensor(dst[:, t, :], window[:].indirect(pos1_sb[:]), bp[g][:, t, :], ALU.subtract)
+
+        bp = [pick_b(0)]
+        v3_words = gather_words("v3_words", tab3_sb, offs3_sb)
+        v_scales = gather_bytes("v_scales", tab_plane, offs_sb)
+        w3_bf = keep.tile([P, PACK * BANK], BF16, name="w3_bf", tag="bp1", align_bytes=64)
+        w3_q = [quantize("w3_0", round_dealt(w3_bf, w3_raw[0], "scalar"))]
+        bp.append(pick_b(1))
+        w3_q.append(quantize("w3_1", round_dealt(new_rounded("w3_bf", 0), w3_raw[1], "scalar")))
+
+        w1_raw = {}
+        w1_raw[0, 0] = w1_block(0, 0, "C")
+        tab_sb = [load_table("tab_sb", tab_words[0], 0)]
+        w1_raw[0, 1] = w1_block(0, 1, "D")
+        tab_sb.append(load_table("tab_sb", tab_words[1], 1))
+        w1_raw[1, 1] = w1_block(1, 1, "B")
+        w1_raw[1, 0] = w1_block(1, 0, "A")
+        pos1_sb = load_list("pos1_sb", pos1)
+        w1_q = {(0, 0): quantize("w1_00", round_dealt(new_rounded("w1_bf", 1), w1_raw[0, 0], "vector"))}
+
+        v_words = [gather_words("v_words0", tab_sb[0], offs_sb)]
+        pair = [tables.tile([P, 2, PACK, PICKS], F32, name="pair0", tag="table0", align_bytes=64)]
+        pick_d(0, pair[0][:, 0])
+        w1_q[0, 1] = quantize("w1_01", round_dealt(new_rounded("w1_bf", 2), w1_raw[0, 1], "scalar"))
+        v_words.append(gather_words("v_words1", tab_sb[1], offs_sb))
+        pair.append(tables.tile([P, 2, PACK, PICKS], F32, name="pair1", tag="table1", align_bytes=64))
+        pick_d(1, pair[1][:, 0])
+        w1_q[1, 1] = quantize("w1_11", round_dealt(new_rounded("w1_bf", 0), w1_raw[1, 1], "scalar"))
+        w1_q[1, 0] = quantize("w1_10", round_dealt(new_rounded("w1_bf", 3), w1_raw[1, 0], "vector"))
+        w5_raw = [load_raw("w5_raw", w5[PASS * g : PASS * g + PASS, :], "CE"[g]) for g in range(2)]
         w4_sb = keep.tile([P, 2, 2 * N], U8, name="w4_sb", align_bytes=64)
         nc.sync.dma_start(w4_sb[:].bitcast(I32), w4_words.rearrange("a p n -> p a n").bitcast(I32))
         for q in range(QUADS):
@@ -223,42 +243,68 @@ def tile_list_shade_finder_contrast_kernel(
         bo_sb = lists.tile([P, N // P], F32, name="bo_sb")
         with nc.allow_non_contiguous_dma(reason="one bias value a partition"):
             nc.sync.dma_start(bo_sb[:], bo.rearrange("(c p) -> p c", p=P))
-        w5_q = [quantize("w5_%d" % g, round_woven(new_rounded("w5_bf"), w5_raw[g])) for g in range(2)]
+        w5_q = {1: quantize("w5_1", round_woven(new_rounded("w5_bf", 1), w5_raw[1][:], "vector"))}
 
-        final = [psum.tile([P, PICKS], F32, name="final%d" % c, tag="final") for c in range(N // P)]
-        diff = []
+        HALF = PICKS // 2
+        def z_part(g, toks, slot, z_codes, z_scales):
+            width = toks.stop - toks.start
+            z_bf = (rows if g else rounded).tile([P, PACK * width], BF16, name="z_bf", tag=("rows9" if g else "rounded2"), align_bytes=64)
+            nc.vector.tensor_tensor(woven_out(z_bf), woven_in(pair[g][:, 1, :, toks]), woven_in(fac[g][:, :, toks]), ALU.mult)
+            nc.vector.quantize_mx(out=z_codes[:, toks].bitcast(FP8X4), scales=z_scales[:, toks], in_=z_bf[:])
+
+        def z_passes(g, h, z_codes, z_scales):
+            for c in range(N // P):
+                for e in range(HALF // P):
+                    toks = slice(HALF * h + P * e, HALF * h + P * e + P)
+                    nc.tensor.matmul_mx(
+                        out=final[h, c // 2][:, c % 2, P * e : P * e + P],
+                        lhsT=w4_sb[:, g, 2 * P * c : 2 * P * c + 2 * P].bitcast(FP4X4),
+                        lhsT_scale=w4_plane[:, N * g + P * c : N * g + P * c + P],
+                        rhs=z_codes[:, toks].bitcast(FP8X4), rhs_scale=z_scales[:, toks],
+                        start=(g == 0 and c % 2 == 0 and e == 0), stop=(g == 1 and c % 2 == 1 and e == 1),
+                    )
+
+        def z_tiles(g):
+            return (
+                keep.tile([P, PICKS], U32, name="z_codes%d" % g, align_bytes=64),
+                keep.tile([P, PICKS], U8, name="z_scales%d" % g, align_bytes=64),
+            )
+
+        fac = [damped_lamp(0)]
+        pick_a(0, pair[0][:, 1])
+        z_codes, z_scales = z_tiles(0)
+        z_part(0, slice(0, PICKS), 2, z_codes, z_scales)
+        fac.append(damped_lamp(1))
+        pick_a(1, pair[1][:, 1])
+        final = {
+            (h, u): psum.tile([P, 2, HALF], F32, name="final%d%d" % (h, u), tag="bank%d" % (4 + 2 * h + u)) for h in range(2) for u in range(2)
+        }
+        for h in range(2):
+            z_passes(0, h, z_codes, z_scales)
+        w5_q[0] = quantize("w5_0", round_woven(new_rounded("w5_bf", 3), w5_raw[0][:], "scalar"))
         for g in range(2):
-            diff.append(keep.tile([P, PACK, PICKS], F32, name="diff%d" % g))
-            for t in range(PACK):
-                passes = [(w1_q[2 * g + a][0], w1_q[2 * g + a][1], v_words[a], v_scales, 4 * a) for a in range(2)]
-                window = first_stage("a_rows", passes, t, None)
-                nc.vector.tensor_tensor(diff[g][:, t, :], window[:].indirect(pos1_sb[:]), bp[g][:, t, :], ALU.subtract)
-        for g in range(2):
-            nc.vector.tensor_tensor(fac[g][:], fac[g][:], dp[g][:], ALU.mult)
-            dp_bf = new_rounded("dp_bf")
-            nc.scalar.copy(woven_out(dp_bf), woven_in(dp[g][:]))
-            dp_codes, dp_scales = quantize("dp_%d" % g, dp_bf)
+            dp_codes, dp_scales = quantize("dp_%d" % g, round_woven(rows.tile([P, PACK * BANK], BF16, name="dp_bf", tag="rows%d" % (8 + g), align_bytes=64), pair[g][:, 0], "scalar"))
             w5_codes, w5_scales = w5_q[g]
-            for c in range(N // P):
-                cols = slice(P * c, P * c + P)
-                nc.tensor.matmul_mx(
-                    out=final[c][:], lhsT=w5_codes[:, cols].bitcast(FP8X4), lhsT_scale=w5_scales[:, cols],
-                    rhs=dp_codes[:].bitcast(FP8X4), rhs_scale=dp_scales[:], start=(g == 0), stop=False,
+            for h in range(2):
+                toks = slice(HALF * h, HALF * (h + 1))
+                for c in range(N // P):
+                    cols = slice(P * c, P * c + P)
+                    nc.tensor.matmul_mx(
+                        out=final[h, c // 2][:, c % 2, :], lhsT=w5_codes[:, cols].bitcast(FP8X4), lhsT_scale=w5_scales[:, cols],
+                        rhs=dp_codes[:, toks].bitcast(FP8X4), rhs_scale=dp_scales[:, toks], start=False, stop=False,
+                    )
+        z_codes, z_scales = z_tiles(1)
+        for h in range(2):
+            z_part(1, slice(HALF * h, HALF * (h + 1)), 1, z_codes, z_scales)
+            z_passes(1, h, z_codes, z_scales)
+            for u in range(2):
+                result = rows.tile([P, 2, HALF], F32, name="result", tag=next_tag("rows", 12), align_bytes=64)
+                for e in range(2):
+                    c = 2 * u + e
+                    if h == 1 and u == 1:
+                        nc.vector.tensor_scalar(result[:, e, :], final[h, u][:, e, :], bo_sb[:, c : c + 1], None, ALU.add)
+                    else:
+                        nc.scalar.activation(result[:, e, :], final[h, u][:, e, :], ACT.Identity, bias=bo_sb[:, c : c + 1])
+                nc.sync.dma_start(
+                    out[2 * P * u : 2 * P * (u + 1), HALF * h : HALF * (h + 1)].rearrange("(e p) n -> p e n", p=P), result[:]
                 )
-        for g in range(2):
-            z_bf = new_rounded("z_bf")
-            nc.vector.tensor_tensor(woven_out(z_bf), woven_in(diff[g][:]), woven_in(fac[g][:]), ALU.mult)
-            z_codes, z_scales = quantize("z_%d" % g, z_bf)
-            for c in range(N // P):
-                nc.tensor.matmul_mx(
-                    out=final[c][:], lhsT=w4_sb[:, g, 2 * P * c : 2 * P * c + 2 * P].bitcast(FP4X4),
-                    lhsT_scale=w4_plane[:, N * g + P * c : N * g + P * c + P],
-                    rhs=z_codes[:].bitcast(FP8X4), rhs_scale=z_scales[:], start=False, stop=(g == 1),
-                )
-        for c in range(N // P):
-            result = results.tile([P, PICKS], F32, name="result")
-            if c % 2 == 0:
-                nc.scalar.activation(result[:], final[c][:], ACT.Identity, bias=bo_sb[:, c : c + 1])
-            else:
-                nc.vector.tensor_scalar(result[:], final[c][:], bo_sb[:, c : c + 1], None, ALU.add)
-            nc.sync.dma_start(out[P * c : P * c + P, :], result[:])

@@ -19,8 +19,13 @@ ACT = mybir.ActivationFunctionType
 P = 128
 PACK = 4
 PASS = P * PACK
+GROUPS = H // PASS
 BANK = 512
+BANKS = 8
 QUADS = 4
+HALF = PICKS // 2
+ROW_SLOTS = 12
+V2_FIRST, V3_FIRST = 8, 12
 
 
 def tile_list_shade_finder_contrast_kernel(
@@ -33,43 +38,45 @@ def tile_list_shade_finder_contrast_kernel(
         lists = ctx.enter_context(tc.tile_pool(name="lists", bufs=1))
         keep = ctx.enter_context(tc.tile_pool(name="keep", bufs=1))
         tables = ctx.enter_context(tc.tile_pool(name="tables", bufs=1))
-        raws = ctx.enter_context(tc.tile_pool(name="raws", bufs=1))
+        blocks = ctx.enter_context(tc.tile_pool(name="blocks", bufs=1))
         rounded = ctx.enter_context(tc.tile_pool(name="rounded", bufs=1))
         rows = ctx.enter_context(tc.tile_pool(name="rows", bufs=1))
         psum = ctx.enter_context(tc.psum_pool(name="psum", bufs=1))
+        taken = {"rows": 0, "bank": 0}
 
-        used = {"raw": 0, "rounded": 0, "rows": 0, "bank": 0}
-
-        def next_tag(kind, slots):
-            used[kind] = used[kind] + 1
-            return "%s%d" % (kind, (used[kind] - 1) % slots)
+        def next_slot(kind, slots):
+            taken[kind] = taken[kind] + 1
+            return "%s%d" % (kind, (taken[kind] - 1) % slots)
 
         def load_list(name, dram):
             tile = lists.tile(list(dram.shape), U16, name=name)
             nc.sync.dma_start(tile[:], dram)
             return tile
 
-        def zeroed_bytes(name, shape):
-            tile = keep.tile(shape, U8, name=name, align_bytes=64)
+        def zeroed_plane(name, width):
+            tile = keep.tile([P, width], U8, name=name, align_bytes=64)
             nc.vector.memset(tile[:].bitcast(I32), 0)
             return tile
 
-        def load_scale_rows(tile, dram, first):
+        def load_scale_rows(plane, dram, first):
             passes = dram.shape[0]
             for q in range(QUADS):
                 lo = 32 * q + first
                 src = dram[:, 4 * q : 4 * q + 4, :] if passes > 1 else dram[0, 4 * q : 4 * q + 4, :]
-                nc.sync.dma_start(tile[lo : lo + 4 * passes, :].bitcast(I32), src.bitcast(I32))
+                nc.sync.dma_start(plane[lo : lo + 4 * passes, :].bitcast(I32), src.bitcast(I32))
 
         def load_table(name, dram, slot):
             tile = tables.tile([P, T], I32, name=name, tag="table%d" % slot, align_bytes=64)
             nc.sync.dma_start(tile[:], dram.rearrange("p t i -> p (t i)").bitcast(I32))
             return tile
 
-        def load_raw(name, dram, slot):
-            tile = raws.tile([P, PACK, BANK], F32, name=name, tag="raw" + slot)
+        def load_block(name, dram, slot):
+            tile = blocks.tile([P, PACK, BANK], F32, name=name, tag="block" + slot)
             nc.sync.dma_start(tile[:], dram.rearrange("(p j) c -> p j c", j=PACK))
             return tile
+
+        def load_w1(g, a, slot):
+            return load_block("w1_block", w1[PASS * a : PASS * a + PASS, PASS * g : PASS * g + PASS], slot)
 
         def gather_words(name, table, offsets):
             tile = keep.tile([P, S], U32, name=name, align_bytes=64)
@@ -81,7 +88,7 @@ def tile_list_shade_finder_contrast_kernel(
             nc.vector.tensor_copy(tile[:], plane[:].indirect(offsets[:]))
             return tile
 
-        def new_rounded(name, slot):
+        def rounded_tile(name, slot):
             return rounded.tile([P, PACK * BANK], BF16, name=name, tag="rounded%d" % slot, align_bytes=64)
 
         def woven_out(dst):
@@ -90,169 +97,183 @@ def tile_list_shade_finder_contrast_kernel(
         def woven_in(src):
             return src.rearrange("p j (c i) -> p c j i", i=4)
 
-        def copy_on(engine, o, i):
-            if engine == "scalar":
-                nc.scalar.copy(o, i)
-            else:
-                nc.vector.tensor_copy(o, i)
+        def round_woven(dst, src, copy):
+            copy(woven_out(dst), woven_in(src))
+            return dst
 
-        def round_dealt(dst, raw, engine):
-            copy_on(
-                engine,
+        def round_dealt(dst, block, copy):
+            copy(
                 dst[:].rearrange("p (t m j) -> p m j t", t=PACK, j=PACK),
-                raw[:].rearrange("p j (m t) -> p m j t", t=PACK),
+                block[:].rearrange("p j (m t) -> p m j t", t=PACK),
             )
             return dst
 
-        def round_woven(dst, src, engine):
-            copy_on(engine, woven_out(dst), woven_in(src))
-            return dst
-
-        def quantize(name, src):
+        def mx_tiles(name):
             codes = keep.tile([P, BANK], U32, name=name + "_codes", align_bytes=64)
             scales = keep.tile([P, BANK], U8, name=name + "_scales", align_bytes=64)
+            return codes, scales
+
+        def quantize(name, src):
+            codes, scales = mx_tiles(name)
             nc.vector.quantize_mx(out=codes[:].bitcast(FP8X4), scales=scales[:], in_=src[:])
             return codes, scales
 
         def first_stage(name, passes, t, bias):
             cols = slice(P * t, P * t + P)
-            window = rows.tile([P, S], F32, name=name, tag=next_tag("rows", 12), align_bytes=64)
-            for h in range(S // BANK):
-                half = slice(BANK * h, BANK * h + BANK)
-                acc = psum.tile([P, BANK], F32, name=name + "_acc", tag=next_tag("bank", 8))
+            window = rows.tile([P, S], F32, name=name, tag=next_slot("rows", ROW_SLOTS), align_bytes=64)
+            for lo in range(0, S, BANK):
+                part = slice(lo, lo + BANK)
+                acc = psum.tile([P, BANK], F32, name=name + "_acc", tag=next_slot("bank", BANKS))
                 for a, (codes, scales, words, plane, first) in enumerate(passes):
                     nc.tensor.matmul_mx(
                         out=acc[:], lhsT=codes[:, cols].bitcast(FP8X4), lhsT_scale=scales[:, cols],
-                        rhs=words[:, half].bitcast(FP8X4), rhs_scale=plane[first:P, half],
+                        rhs=words[:, part].bitcast(FP8X4), rhs_scale=plane[first:P, part],
                         start=(a == 0), stop=(a == len(passes) - 1),
                     )
                 if bias is None:
-                    nc.scalar.copy(window[:, half], acc[:])
+                    nc.scalar.copy(window[:, part], acc[:])
                 else:
-                    nc.scalar.activation(window[:, half], acc[:], ACT.Identity, bias=bias)
+                    nc.scalar.activation(window[:, part], acc[:], ACT.Identity, bias=bias)
             return window
 
-        def w1_block(g, a, slot):
-            return load_raw("w1_raw", w1[PASS * a : PASS * a + PASS, BANK * g : BANK * g + BANK], slot)
+        on_scalar, on_vector = nc.scalar.copy, nc.vector.tensor_copy
 
-        tab2_plane = zeroed_bytes("tab2_plane", [P, T])
-        w2_plane = zeroed_bytes("w2_plane", [P, H])
-        tab3_plane = zeroed_bytes("tab3_plane", [P, T])
-        tab_plane = zeroed_bytes("tab_plane", [P, T])
-        w4_plane = zeroed_bytes("w4_plane", [P, 2 * N])
+        warm = keep.tile([P, 1], F32, name="warm")
+        nc.vector.memset(warm[:], 1.0)
+        nc.scalar.activation(warm[:], warm[:], ACT.Abs_reciprocal_sqrt)
+
+        tab2_plane = zeroed_plane("tab2_plane", T)
+        w2_plane = zeroed_plane("w2_plane", H)
+        tab3_plane = zeroed_plane("tab3_plane", T)
+        tab_plane = zeroed_plane("tab_plane", T)
+        w4_plane = zeroed_plane("w4_plane", GROUPS * N)
 
         offs2_sb = load_list("offs2_sb", offs2)
         w2_sb = keep.tile([P, H], I32, name="w2_sb", align_bytes=64)
         nc.sync.dma_start(w2_sb[:], w2_words[0].rearrange("p c i -> p (c i)").bitcast(I32))
-        load_scale_rows(tab2_plane, tab2_scales, 8)
+        load_scale_rows(tab2_plane, tab2_scales, V2_FIRST)
         tab2_sb = load_table("tab2_sb", tab2_words[0], 0)
         load_scale_rows(w2_plane, w2_scales, 0)
         offs3_sb = load_list("offs3_sb", offs3)
-        load_scale_rows(tab3_plane, tab3_scales, 12)
+        load_scale_rows(tab3_plane, tab3_scales, V3_FIRST)
         pos2_sb = load_list("pos2_sb", pos2)
         tab3_sb = load_table("tab3_sb", tab3_words[0], 1)
         offs_sb = load_list("offs_sb", offs)
         load_scale_rows(tab_plane, tab_scales, 0)
-        w3_raw = [load_raw("w3_raw", w3[:, BANK * g : BANK * g + BANK], "AB"[g]) for g in range(2)]
-        bd_sb = lists.tile([P, 2, PACK], F32, name="bd_sb")
+        w3_blocks = [load_block("w3_block", w3[:, PASS * g : PASS * g + PASS], "AB"[g]) for g in range(GROUPS)]
+        bd_sb = lists.tile([P, GROUPS, PACK], F32, name="bd_sb")
         nc.sync.dma_start(bd_sb[:], bd.rearrange("(g p t) -> p g t", p=P, t=PACK))
         pos3_sb = load_list("pos3_sb", pos3)
 
         v2_scales = gather_bytes("v2_scales", tab2_plane, offs2_sb)
         w2_codes = keep.tile([P, H], I32, name="w2_codes", align_bytes=64)
         nc.vector.tensor_copy(
-            w2_codes[:].rearrange("p (g t m) -> p g m t", g=2, t=PACK),
-            w2_sb[:].rearrange("p (g m t) -> p g m t", g=2, t=PACK),
+            w2_codes[:].rearrange("p (g t m) -> p g m t", g=GROUPS, t=PACK),
+            w2_sb[:].rearrange("p (g m t) -> p g m t", g=GROUPS, t=PACK),
         )
         v2_words = gather_words("v2_words", tab2_sb, offs2_sb)
         w2_dealt = keep.tile([P, H], U8, name="w2_dealt", align_bytes=64)
         nc.vector.tensor_copy(
-            w2_dealt[:].rearrange("p (g t m) -> p g t m", g=2, t=PACK),
-            w2_plane[:].rearrange("p (g m t) -> p g t m", g=2, t=PACK),
+            w2_dealt[:].rearrange("p (g t m) -> p g t m", g=GROUPS, t=PACK),
+            w2_plane[:].rearrange("p (g m t) -> p g t m", g=GROUPS, t=PACK),
         )
         v3_scales = gather_bytes("v3_scales", tab3_plane, offs3_sb)
 
         def pick_b(g):
-            gc = slice(BANK * g, BANK * g + BANK)
-            tile = keep.tile([P, PACK, PICKS], F32, name="bp%d" % g, tag="bp%d" % g, align_bytes=64)
+            cols = slice(PASS * g, PASS * g + PASS)
+            passes = [(w2_codes[:, cols], w2_dealt[:, cols], v2_words, v2_scales, V2_FIRST)]
+            pairs = [
+                keep.tile([P, 2, PICKS], F32, name="bp%d%d" % (g, u), tag="bp%d%d" % (g, u), align_bytes=64)
+                for u in range(PACK // 2)
+            ]
             for t in range(PACK):
-                window = first_stage("b_rows", [(w2_codes[:, gc], w2_dealt[:, gc], v2_words, v2_scales, 8)], t, None)
-                nc.vector.tensor_copy(tile[:, t, :], window[:].indirect(pos2_sb[:]))
-            return tile
+                window = first_stage("b_rows", passes, t, None)
+                nc.vector.tensor_copy(pairs[t // 2][:, t % 2, :], window[:].indirect(pos2_sb[:]))
+            return pairs
 
-        def damping(g):
-            tile = raws.tile([P, PACK, PICKS], F32, name="fac%d" % g, tag="raw" + "DB"[g])
-            nc.scalar.activation(tile[:], bp[g][:], ACT.Abs)
-            nc.scalar.activation(tile[:], tile[:], ACT.Abs_reciprocal_sqrt, bias=1.0)
-            nc.scalar.activation(tile[:], tile[:], ACT.Square)
-            return tile
-
-        def damped_lamp(g):
-            damp = damping(g)
-            tile = raws.tile([P, PACK, PICKS], F32, name="wt%d" % g, tag="raw" + "AE"[g])
-            nc.vector.tensor_tensor(tile[:], damp[:], pair[g][:, 0], ALU.mult)
-            return tile
-
-        def pick_d(g, dst):
-            codes, scales = w3_q[g]
+        def pick_d(g):
+            both = tables.tile([P, 2, PACK, PICKS], F32, name="picked%d" % g, tag="table%d" % g, align_bytes=64)
+            passes = [w3_mx[g] + (v3_words, v3_scales, V3_FIRST)]
             for t in range(PACK):
-                window = first_stage("d_rows", [(codes, scales, v3_words, v3_scales, 12)], t, bd_sb[:, g, t : t + 1])
-                nc.vector.tensor_copy(dst[:, t, :], window[:].indirect(pos3_sb[:]))
+                window = first_stage("d_rows", passes, t, bd_sb[:, g, t : t + 1])
+                nc.vector.tensor_copy(both[:, 0, t, :], window[:].indirect(pos3_sb[:]))
+            return both
 
-        def pick_a(g, dst):
-            passes = [(w1_q[g, a][0], w1_q[g, a][1], v_words[a], v_scales, 4 * a) for a in range(2)]
+        def pick_a_minus_b(g):
+            passes = [w1_mx[g, a] + (v_words[a], v_scales, 4 * a) for a in range(K // PASS)]
             for t in range(PACK):
                 window = first_stage("a_rows", passes, t, None)
-                nc.vector.tensor_tensor(dst[:, t, :], window[:].indirect(pos1_sb[:]), bp[g][:, t, :], ALU.subtract)
+                nc.vector.tensor_tensor(
+                    picked[g][:, 1, t, :], window[:].indirect(pos1_sb[:]), bp[g][t // 2][:, t % 2, :], ALU.subtract
+                )
+
+        def damped_lamp(g, damp_slot, product_slot):
+            damp = blocks.tile([P, PACK, PICKS], F32, name="damp%d" % g, tag="block" + damp_slot)
+            for u in range(PACK // 2):
+                nc.scalar.activation(damp[:, 2 * u : 2 * u + 2, :], bp[g][u][:], ACT.Abs)
+            nc.scalar.activation(damp[:], damp[:], ACT.Abs_reciprocal_sqrt, bias=1.0)
+            nc.scalar.activation(damp[:], damp[:], ACT.Square)
+            product = blocks.tile([P, PACK, PICKS], F32, name="lamp%d" % g, tag="block" + product_slot)
+            nc.vector.tensor_tensor(product[:], damp[:], picked[g][:, 0], ALU.mult)
+            return product
+
+        def quantize_z(g, toks, z_bf, z_mx):
+            nc.vector.tensor_tensor(
+                woven_out(z_bf), woven_in(picked[g][:, 1, :, toks]), woven_in(lamp[g][:, :, toks]), ALU.mult
+            )
+            nc.vector.quantize_mx(out=z_mx[0][:, toks].bitcast(FP8X4), scales=z_mx[1][:, toks], in_=z_bf[:])
 
         bp = [pick_b(0)]
         v3_words = gather_words("v3_words", tab3_sb, offs3_sb)
         v_scales = gather_bytes("v_scales", tab_plane, offs_sb)
-        w3_bf = keep.tile([P, PACK * BANK], BF16, name="w3_bf", tag="bp1", align_bytes=64)
-        w3_q = [quantize("w3_0", round_dealt(w3_bf, w3_raw[0], "scalar"))]
+        w3_bf = keep.tile([P, PACK * BANK], BF16, name="w3_bf", tag="bp11", align_bytes=64)
+        w3_mx = [quantize("w3_0", round_dealt(w3_bf, w3_blocks[0], on_scalar))]
         bp.append(pick_b(1))
-        w3_q.append(quantize("w3_1", round_dealt(new_rounded("w3_bf", 0), w3_raw[1], "scalar")))
+        w3_mx.append(quantize("w3_1", round_dealt(rounded_tile("w3_bf", 0), w3_blocks[1], on_scalar)))
 
-        w1_raw = {}
-        w1_raw[0, 0] = w1_block(0, 0, "C")
+        w1_blocks = {(0, 0): load_w1(0, 0, "C")}
         tab_sb = [load_table("tab_sb", tab_words[0], 0)]
-        w1_raw[0, 1] = w1_block(0, 1, "D")
+        w1_blocks[0, 1] = load_w1(0, 1, "D")
         tab_sb.append(load_table("tab_sb", tab_words[1], 1))
-        w1_raw[1, 1] = w1_block(1, 1, "B")
-        w1_raw[1, 0] = w1_block(1, 0, "A")
+        w1_blocks[1, 1] = load_w1(1, 1, "B")
+        w1_blocks[1, 0] = load_w1(1, 0, "A")
         pos1_sb = load_list("pos1_sb", pos1)
-        w1_q = {(0, 0): quantize("w1_00", round_dealt(new_rounded("w1_bf", 1), w1_raw[0, 0], "vector"))}
-
+        w1_mx = {(0, 0): quantize("w1_00", round_dealt(rounded_tile("w1_bf", 1), w1_blocks[0, 0], on_vector))}
         v_words = [gather_words("v_words0", tab_sb[0], offs_sb)]
-        pair = [tables.tile([P, 2, PACK, PICKS], F32, name="pair0", tag="table0", align_bytes=64)]
-        pick_d(0, pair[0][:, 0])
-        w1_q[0, 1] = quantize("w1_01", round_dealt(new_rounded("w1_bf", 2), w1_raw[0, 1], "scalar"))
+        picked = [pick_d(0)]
+        w1_mx[0, 1] = quantize("w1_01", round_dealt(rounded_tile("w1_bf", 2), w1_blocks[0, 1], on_scalar))
         v_words.append(gather_words("v_words1", tab_sb[1], offs_sb))
-        pair.append(tables.tile([P, 2, PACK, PICKS], F32, name="pair1", tag="table1", align_bytes=64))
-        pick_d(1, pair[1][:, 0])
-        w1_q[1, 1] = quantize("w1_11", round_dealt(new_rounded("w1_bf", 0), w1_raw[1, 1], "scalar"))
-        w1_q[1, 0] = quantize("w1_10", round_dealt(new_rounded("w1_bf", 3), w1_raw[1, 0], "vector"))
-        w5_raw = [load_raw("w5_raw", w5[PASS * g : PASS * g + PASS, :], "CE"[g]) for g in range(2)]
-        w4_sb = keep.tile([P, 2, 2 * N], U8, name="w4_sb", align_bytes=64)
+        picked.append(pick_d(1))
+        w1_mx[1, 1] = quantize("w1_11", round_dealt(rounded_tile("w1_bf", 0), w1_blocks[1, 1], on_vector))
+        w1_mx[1, 0] = quantize("w1_10", round_dealt(rounded_tile("w1_bf", 3), w1_blocks[1, 0], on_vector))
+
+        w5_blocks = [load_block("w5_block", w5[PASS * g : PASS * g + PASS, :], "CE"[g]) for g in range(GROUPS)]
+        w4_sb = keep.tile([P, GROUPS, 2 * N], U8, name="w4_sb", align_bytes=64)
         nc.sync.dma_start(w4_sb[:].bitcast(I32), w4_words.rearrange("a p n -> p a n").bitcast(I32))
         for q in range(QUADS):
             nc.sync.dma_start(
-                w4_plane[32 * q : 32 * q + 4, :].rearrange("r (a n) -> r a n", a=2).bitcast(I32),
+                w4_plane[32 * q : 32 * q + 4, :].rearrange("r (a n) -> r a n", a=GROUPS).bitcast(I32),
                 w4_scales[:, 4 * q : 4 * q + 4, :].rearrange("a r n -> r a n").bitcast(I32),
             )
         bo_sb = lists.tile([P, N // P], F32, name="bo_sb")
         with nc.allow_non_contiguous_dma(reason="one bias value a partition"):
             nc.sync.dma_start(bo_sb[:], bo.rearrange("(c p) -> p c", p=P))
-        w5_q = {1: quantize("w5_1", round_woven(new_rounded("w5_bf", 1), w5_raw[1][:], "vector"))}
+        w5_mx = {1: quantize("w5_1", round_woven(rounded_tile("w5_bf", 1), w5_blocks[1][:], on_vector))}
 
-        HALF = PICKS // 2
-        def z_part(g, toks, slot, z_codes, z_scales):
-            width = toks.stop - toks.start
-            z_bf = (rows if g else rounded).tile([P, PACK * width], BF16, name="z_bf", tag=("rows9" if g else "rounded2"), align_bytes=64)
-            nc.vector.tensor_tensor(woven_out(z_bf), woven_in(pair[g][:, 1, :, toks]), woven_in(fac[g][:, :, toks]), ALU.mult)
-            nc.vector.quantize_mx(out=z_codes[:, toks].bitcast(FP8X4), scales=z_scales[:, toks], in_=z_bf[:])
+        lamp = [damped_lamp(0, "D", "A")]
+        pick_a_minus_b(0)
+        z_mx = mx_tiles("z_0")
+        quantize_z(0, slice(0, PICKS), rounded_tile("z_bf", 2), z_mx)
+        lamp.append(damped_lamp(1, "B", "E"))
+        pick_a_minus_b(1)
 
-        def z_passes(g, h, z_codes, z_scales):
+        final = {
+            (h, u): psum.tile([P, 2, HALF], F32, name="final%d%d" % (h, u), tag="bank%d" % (BANKS - 4 + 2 * h + u))
+            for h in range(2)
+            for u in range(2)
+        }
+
+        def z_passes(g, h, z_mx):
             for c in range(N // P):
                 for e in range(HALF // P):
                     toks = slice(HALF * h + P * e, HALF * h + P * e + P)
@@ -260,51 +281,43 @@ def tile_list_shade_finder_contrast_kernel(
                         out=final[h, c // 2][:, c % 2, P * e : P * e + P],
                         lhsT=w4_sb[:, g, 2 * P * c : 2 * P * c + 2 * P].bitcast(FP4X4),
                         lhsT_scale=w4_plane[:, N * g + P * c : N * g + P * c + P],
-                        rhs=z_codes[:, toks].bitcast(FP8X4), rhs_scale=z_scales[:, toks],
-                        start=(g == 0 and c % 2 == 0 and e == 0), stop=(g == 1 and c % 2 == 1 and e == 1),
+                        rhs=z_mx[0][:, toks].bitcast(FP8X4), rhs_scale=z_mx[1][:, toks],
+                        start=(g == 0 and c % 2 == 0 and e == 0),
+                        stop=(g == GROUPS - 1 and c % 2 == 1 and e == HALF // P - 1),
                     )
 
-        def z_tiles(g):
-            return (
-                keep.tile([P, PICKS], U32, name="z_codes%d" % g, align_bytes=64),
-                keep.tile([P, PICKS], U8, name="z_scales%d" % g, align_bytes=64),
-            )
+        def a_row_slot(t):
+            return "rows%d" % ((2 * GROUPS * PACK + t) % ROW_SLOTS)
 
-        fac = [damped_lamp(0)]
-        pick_a(0, pair[0][:, 1])
-        z_codes, z_scales = z_tiles(0)
-        z_part(0, slice(0, PICKS), 2, z_codes, z_scales)
-        fac.append(damped_lamp(1))
-        pick_a(1, pair[1][:, 1])
-        final = {
-            (h, u): psum.tile([P, 2, HALF], F32, name="final%d%d" % (h, u), tag="bank%d" % (4 + 2 * h + u)) for h in range(2) for u in range(2)
-        }
         for h in range(2):
-            z_passes(0, h, z_codes, z_scales)
-        w5_q[0] = quantize("w5_0", round_woven(new_rounded("w5_bf", 3), w5_raw[0][:], "scalar"))
-        for g in range(2):
-            dp_codes, dp_scales = quantize("dp_%d" % g, round_woven(rows.tile([P, PACK * BANK], BF16, name="dp_bf", tag="rows%d" % (8 + g), align_bytes=64), pair[g][:, 0], "scalar"))
-            w5_codes, w5_scales = w5_q[g]
+            z_passes(0, h, z_mx)
+        w5_mx[0] = quantize("w5_0", round_woven(rounded_tile("w5_bf", 3), w5_blocks[0][:], on_scalar))
+        for g in range(GROUPS):
+            dp_bf = rows.tile([P, PACK * PICKS], BF16, name="dp_bf", tag=a_row_slot(g), align_bytes=64)
+            dp_codes, dp_scales = quantize("dp_%d" % g, round_woven(dp_bf, picked[g][:, 0], on_scalar))
             for h in range(2):
-                toks = slice(HALF * h, HALF * (h + 1))
+                toks = slice(HALF * h, HALF * h + HALF)
                 for c in range(N // P):
                     cols = slice(P * c, P * c + P)
                     nc.tensor.matmul_mx(
-                        out=final[h, c // 2][:, c % 2, :], lhsT=w5_codes[:, cols].bitcast(FP8X4), lhsT_scale=w5_scales[:, cols],
-                        rhs=dp_codes[:, toks].bitcast(FP8X4), rhs_scale=dp_scales[:, toks], start=False, stop=False,
+                        out=final[h, c // 2][:, c % 2, :],
+                        lhsT=w5_mx[g][0][:, cols].bitcast(FP8X4), lhsT_scale=w5_mx[g][1][:, cols],
+                        rhs=dp_codes[:, toks].bitcast(FP8X4), rhs_scale=dp_scales[:, toks],
+                        start=False, stop=False,
                     )
-        z_codes, z_scales = z_tiles(1)
+
+        z_mx = mx_tiles("z_1")
         for h in range(2):
-            z_part(1, slice(HALF * h, HALF * (h + 1)), 1, z_codes, z_scales)
-            z_passes(1, h, z_codes, z_scales)
+            toks = slice(HALF * h, HALF * h + HALF)
+            z_bf = rows.tile([P, PACK * HALF], BF16, name="z_bf", tag=a_row_slot(h), align_bytes=64)
+            quantize_z(1, toks, z_bf, z_mx)
+            z_passes(1, h, z_mx)
             for u in range(2):
-                result = rows.tile([P, 2, HALF], F32, name="result", tag=next_tag("rows", 12), align_bytes=64)
+                result = rows.tile([P, 2, HALF], F32, name="result", tag=next_slot("rows", ROW_SLOTS), align_bytes=64)
                 for e in range(2):
-                    c = 2 * u + e
-                    if h == 1 and u == 1:
-                        nc.vector.tensor_scalar(result[:, e, :], final[h, u][:, e, :], bo_sb[:, c : c + 1], None, ALU.add)
+                    bias = bo_sb[:, 2 * u + e : 2 * u + e + 1]
+                    if (h, u) == (1, 1):
+                        nc.vector.tensor_scalar(result[:, e, :], final[h, u][:, e, :], bias, None, ALU.add)
                     else:
-                        nc.scalar.activation(result[:, e, :], final[h, u][:, e, :], ACT.Identity, bias=bo_sb[:, c : c + 1])
-                nc.sync.dma_start(
-                    out[2 * P * u : 2 * P * (u + 1), HALF * h : HALF * (h + 1)].rearrange("(e p) n -> p e n", p=P), result[:]
-                )
+                        nc.scalar.activation(result[:, e, :], final[h, u][:, e, :], ACT.Identity, bias=bias)
+                nc.sync.dma_start(out[2 * P * u : 2 * P * u + 2 * P, toks].rearrange("(e p) n -> p e n", p=P), result[:])

@@ -54,7 +54,7 @@ def tile_list_shade_finder_contrast_kernel(
             return tile
 
         def zeroed_plane(name, width):
-            tile = keep.tile([P, width], U8, name=name, align_bytes=64)
+            tile = keep.tile([P, width], U8, name=name, tag=name, align_bytes=64)
             nc.vector.memset(tile[:].bitcast(I32), 0)
             return tile
 
@@ -81,7 +81,13 @@ def tile_list_shade_finder_contrast_kernel(
         def gather_words(name, table, offsets):
             tile = keep.tile([P, S], U32, name=name, align_bytes=64)
             nc.vector.tensor_copy(tile[:], table[:].bitcast(U32).indirect(offsets[:]))
-            return tile
+            return [tile[:, lo : lo + BANK] for lo in range(0, S, BANK)]
+
+        def gather_word_half(name, tag, table, offsets, half):
+            tile = keep.tile([P, BANK], U32, name=name, tag=tag, align_bytes=64)
+            entries = offsets[:, BANK // 16 * half : BANK // 16 * (half + 1)]
+            nc.vector.tensor_copy(tile[:], table[:].bitcast(U32).indirect(entries))
+            return tile[:]
 
         def gather_bytes(name, plane, offsets):
             tile = keep.tile([P, S], U8, name=name, align_bytes=64)
@@ -127,7 +133,7 @@ def tile_list_shade_finder_contrast_kernel(
                 for a, (codes, scales, words, plane, first) in enumerate(passes):
                     nc.tensor.matmul_mx(
                         out=acc[:], lhsT=codes[:, cols].bitcast(FP8X4), lhsT_scale=scales[:, cols],
-                        rhs=words[:, part].bitcast(FP8X4), rhs_scale=plane[first:P, part],
+                        rhs=words[lo // BANK].bitcast(FP8X4), rhs_scale=plane[first:P, part],
                         start=(a == 0), stop=(a == len(passes) - 1),
                     )
                 if bias is None:
@@ -158,9 +164,9 @@ def tile_list_shade_finder_contrast_kernel(
         load_scale_rows(tab3_plane, tab3_scales, V3_FIRST)
         pos2_sb = load_list("pos2_sb", pos2)
         tab3_sb = load_table("tab3_sb", tab3_words[0], 1)
+        w3_blocks = [load_block("w3_block", w3[:, PASS * g : PASS * g + PASS], "AB"[g]) for g in range(GROUPS)]
         offs_sb = load_list("offs_sb", offs)
         load_scale_rows(tab_plane, tab_scales, 0)
-        w3_blocks = [load_block("w3_block", w3[:, PASS * g : PASS * g + PASS], "AB"[g]) for g in range(GROUPS)]
         bd_sb = lists.tile([P, GROUPS, PACK], F32, name="bd_sb")
         nc.sync.dma_start(bd_sb[:], bd.rearrange("(g p t) -> p g t", p=P, t=PACK))
         pos3_sb = load_list("pos3_sb", pos3)
@@ -171,12 +177,13 @@ def tile_list_shade_finder_contrast_kernel(
             w2_codes[:].rearrange("p (g t m) -> p g m t", g=GROUPS, t=PACK),
             w2_sb[:].rearrange("p (g m t) -> p g m t", g=GROUPS, t=PACK),
         )
-        v2_words = gather_words("v2_words", tab2_sb, offs2_sb)
+        v2_words = [gather_word_half("v2_words0", "v2_words0", tab2_sb, offs2_sb, 0)]
         w2_dealt = keep.tile([P, H], U8, name="w2_dealt", align_bytes=64)
         nc.vector.tensor_copy(
             w2_dealt[:].rearrange("p (g t m) -> p g t m", g=GROUPS, t=PACK),
             w2_plane[:].rearrange("p (g m t) -> p g t m", g=GROUPS, t=PACK),
         )
+        v2_words.append(gather_word_half("v2_words1", "w2_plane", tab2_sb, offs2_sb, 1))
         v3_scales = gather_bytes("v3_scales", tab3_plane, offs3_sb)
 
         def pick_b(g):
@@ -209,10 +216,13 @@ def tile_list_shade_finder_contrast_kernel(
 
         def damped_lamp(g, damp_slot, product_slot):
             damp = blocks.tile([P, PACK, PICKS], F32, name="damp%d" % g, tag="block" + damp_slot)
-            for u in range(PACK // 2):
-                nc.scalar.activation(damp[:, 2 * u : 2 * u + 2, :], bp[g][u][:], ACT.Abs)
-            nc.scalar.activation(damp[:], damp[:], ACT.Abs_reciprocal_sqrt, bias=1.0)
-            nc.scalar.activation(damp[:], damp[:], ACT.Square)
+            parts = [damp[:, 2 * u : 2 * u + 2, :] for u in range(PACK // 2)]
+            for part, source in zip(parts, bp[g]):
+                nc.scalar.activation(part, source[:], ACT.Abs)
+            for part in parts:
+                nc.scalar.activation(part, part, ACT.Abs_reciprocal_sqrt, bias=1.0)
+            for part in parts:
+                nc.scalar.activation(part, part, ACT.Square)
             product = blocks.tile([P, PACK, PICKS], F32, name="lamp%d" % g, tag="block" + product_slot)
             nc.vector.tensor_tensor(product[:], damp[:], picked[g][:, 0], ALU.mult)
             return product
@@ -245,7 +255,7 @@ def tile_list_shade_finder_contrast_kernel(
         v_words.append(gather_words("v_words1", tab_sb[1], offs_sb))
         picked.append(pick_d(1))
         w1_mx[1, 1] = quantize("w1_11", round_dealt(rounded_tile("w1_bf", 0), w1_blocks[1, 1], on_vector))
-        w1_mx[1, 0] = quantize("w1_10", round_dealt(rounded_tile("w1_bf", 3), w1_blocks[1, 0], on_vector))
+        w1_mx[1, 0] = quantize("w1_10", round_dealt(rounded_tile("w1_bf", 3), w1_blocks[1, 0], on_scalar))
 
         w5_blocks = [load_block("w5_block", w5[PASS * g : PASS * g + PASS, :], "CE"[g]) for g in range(GROUPS)]
         w4_sb = keep.tile([P, GROUPS, 2 * N], U8, name="w4_sb", align_bytes=64)
@@ -258,7 +268,7 @@ def tile_list_shade_finder_contrast_kernel(
         bo_sb = lists.tile([P, N // P], F32, name="bo_sb")
         with nc.allow_non_contiguous_dma(reason="one bias value a partition"):
             nc.sync.dma_start(bo_sb[:], bo.rearrange("(c p) -> p c", p=P))
-        w5_mx = {1: quantize("w5_1", round_woven(rounded_tile("w5_bf", 1), w5_blocks[1][:], on_vector))}
+        w5_mx = {1: quantize("w5_1", round_woven(rounded_tile("w5_bf", 1), w5_blocks[1][:], on_scalar))}
 
         lamp = [damped_lamp(0, "D", "A")]
         pick_a_minus_b(0)

from contextlib import ExitStack

import concourse.mybir as mybir

K, K2, H, N, T, S, PICKS = 1024, 512, 1024, 512, 4096, 1024, 512
FLOPS = 2 * (K * H * S + 2 * K2 * H * S + 2 * H * N * PICKS)

F32 = mybir.dt.float32
BF16 = mybir.dt.bfloat16
I32 = mybir.dt.int32
U32 = mybir.dt.uint32
U16 = mybir.dt.uint16
U8 = mybir.dt.uint8
FP8X4 = mybir.dt.float8_e4m3fn_x4
FP4X4 = mybir.dt.float4_e2m1fn_x4
ALU = mybir.AluOpType
ACT = mybir.ActivationFunctionType

P = 128
PACK = 4
PASS = P * PACK
GROUPS = H // PASS
BANK = 512
BANKS = 8
QUADS = 4
HALF = PICKS // 2
ROW_SLOTS = 12
V2_FIRST, V3_FIRST = 8, 12


def tile_list_shade_finder_contrast_kernel(
    tc, tab_words, tab_scales, tab2_words, tab2_scales, tab3_words, tab3_scales,
    offs, offs2, offs3, pos1, pos2, pos3,
    w1, w2_words, w2_scales, w3, bd, w4_words, w4_scales, w5, bo, out,
):
    nc = tc.nc
    with ExitStack() as ctx:
        lists = ctx.enter_context(tc.tile_pool(name="lists", bufs=1))
        keep = ctx.enter_context(tc.tile_pool(name="keep", bufs=1))
        tables = ctx.enter_context(tc.tile_pool(name="tables", bufs=1))
        blocks = ctx.enter_context(tc.tile_pool(name="blocks", bufs=1))
        rounded = ctx.enter_context(tc.tile_pool(name="rounded", bufs=1))
        rows = ctx.enter_context(tc.tile_pool(name="rows", bufs=1))
        psum = ctx.enter_context(tc.psum_pool(name="psum", bufs=1))
        taken = {"rows": 0, "bank": 0}

        def next_slot(kind, slots):
            taken[kind] = taken[kind] + 1
            return "%s%d" % (kind, (taken[kind] - 1) % slots)

        def load_list(name, dram):
            tile = lists.tile(list(dram.shape), U16, name=name)
            nc.sync.dma_start(tile[:], dram)
            return tile

        def zeroed_plane(name, width):
            tile = keep.tile([P, width], U8, name=name, tag=name, align_bytes=64)
            nc.vector.memset(tile[:].bitcast(I32), 0)
            return tile

        def load_scale_rows(plane, dram, first):
            passes = dram.shape[0]
            for q in range(QUADS):
                lo = 32 * q + first
                src = dram[:, 4 * q : 4 * q + 4, :] if passes > 1 else dram[0, 4 * q : 4 * q + 4, :]
                nc.sync.dma_start(plane[lo : lo + 4 * passes, :].bitcast(I32), src.bitcast(I32))

        def load_table(name, dram, slot):
            tile = tables.tile([P, T], I32, name=name, tag="table%d" % slot, align_bytes=64)
            nc.sync.dma_start(tile[:], dram.rearrange("p t i -> p (t i)").bitcast(I32))
            return tile

        def load_block(name, dram, slot):
            tile = blocks.tile([P, PACK, BANK], F32, name=name, tag="block" + slot)
            nc.sync.dma_start(tile[:], dram.rearrange("(p j) c -> p j c", j=PACK))
            return tile

        def load_w1(g, a, slot):
            return load_block("w1_block", w1[PASS * a : PASS * a + PASS, PASS * g : PASS * g + PASS], slot)

        def gather_words(name, table, offsets):
            tile = keep.tile([P, S], U32, name=name, align_bytes=64)
            nc.vector.tensor_copy(tile[:], table[:].bitcast(U32).indirect(offsets[:]))
            return [tile[:, lo : lo + BANK] for lo in range(0, S, BANK)]

        def gather_word_half(name, tag, table, offsets, half):
            tile = keep.tile([P, BANK], U32, name=name, tag=tag, align_bytes=64)
            entries = offsets[:, BANK // 16 * half : BANK // 16 * (half + 1)]
            nc.vector.tensor_copy(tile[:], table[:].bitcast(U32).indirect(entries))
            return tile[:]

        def gather_bytes(name, plane, offsets):
            tile = keep.tile([P, S], U8, name=name, align_bytes=64)
            nc.vector.tensor_copy(tile[:], plane[:].indirect(offsets[:]))
            return tile

        def rounded_tile(name, slot):
            return rounded.tile([P, PACK * BANK], BF16, name=name, tag="rounded%d" % slot, align_bytes=64)

        def woven_out(dst):
            return dst[:].rearrange("p (c i j) -> p c j i", i=4, j=PACK)

        def woven_in(src):
            return src.rearrange("p j (c i) -> p c j i", i=4)

        def round_woven(dst, src, copy):
            copy(woven_out(dst), woven_in(src))
            return dst

        def round_dealt(dst, block, copy):
            copy(
                dst[:].rearrange("p (t m j) -> p m j t", t=PACK, j=PACK),
                block[:].rearrange("p j (m t) -> p m j t", t=PACK),
            )
            return dst

        def mx_tiles(name):
            codes = keep.tile([P, BANK], U32, name=name + "_codes", align_bytes=64)
            scales = keep.tile([P, BANK], U8, name=name + "_scales", align_bytes=64)
            return codes, scales

        def quantize(name, src):
            codes, scales = mx_tiles(name)
            nc.vector.quantize_mx(out=codes[:].bitcast(FP8X4), scales=scales[:], in_=src[:])
            return codes, scales

        def first_stage(name, passes, t, bias):
            cols = slice(P * t, P * t + P)
            window = rows.tile([P, S], F32, name=name, tag=next_slot("rows", ROW_SLOTS), align_bytes=64)
            for lo in range(0, S, BANK):
                part = slice(lo, lo + BANK)
                acc = psum.tile([P, BANK], F32, name=name + "_acc", tag=next_slot("bank", BANKS))
                for a, (codes, scales, words, plane, first) in enumerate(passes):
                    nc.tensor.matmul_mx(
                        out=acc[:], lhsT=codes[:, cols].bitcast(FP8X4), lhsT_scale=scales[:, cols],
                        rhs=words[lo // BANK].bitcast(FP8X4), rhs_scale=plane[first:P, part],
                        start=(a == 0), stop=(a == len(passes) - 1),
                    )
                if bias is None:
                    nc.scalar.copy(window[:, part], acc[:])
                else:
                    nc.scalar.activation(window[:, part], acc[:], ACT.Identity, bias=bias)
            return window

        on_scalar, on_vector = nc.scalar.copy, nc.vector.tensor_copy

        warm = keep.tile([P, 1], F32, name="warm")
        nc.vector.memset(warm[:], 1.0)
        nc.scalar.activation(warm[:], warm[:], ACT.Abs_reciprocal_sqrt)

        tab2_plane = zeroed_plane("tab2_plane", T)
        w2_plane = zeroed_plane("w2_plane", H)
        tab3_plane = zeroed_plane("tab3_plane", T)
        tab_plane = zeroed_plane("tab_plane", T)
        w4_plane = zeroed_plane("w4_plane", GROUPS * N)

        offs2_sb = load_list("offs2_sb", offs2)
        w2_sb = keep.tile([P, H], I32, name="w2_sb", align_bytes=64)
        nc.sync.dma_start(w2_sb[:], w2_words[0].rearrange("p c i -> p (c i)").bitcast(I32))
        load_scale_rows(tab2_plane, tab2_scales, V2_FIRST)
        tab2_sb = load_table("tab2_sb", tab2_words[0], 0)
        load_scale_rows(w2_plane, w2_scales, 0)
        offs3_sb = load_list("offs3_sb", offs3)
        load_scale_rows(tab3_plane, tab3_scales, V3_FIRST)
        pos2_sb = load_list("pos2_sb", pos2)
        tab3_sb = load_table("tab3_sb", tab3_words[0], 1)
        w3_blocks = [load_block("w3_block", w3[:, PASS * g : PASS * g + PASS], "AB"[g]) for g in range(GROUPS)]
        offs_sb = load_list("offs_sb", offs)
        load_scale_rows(tab_plane, tab_scales, 0)
        bd_sb = lists.tile([P, GROUPS, PACK], F32, name="bd_sb")
        nc.sync.dma_start(bd_sb[:], bd.rearrange("(g p t) -> p g t", p=P, t=PACK))
        pos3_sb = load_list("pos3_sb", pos3)

        v2_scales = gather_bytes("v2_scales", tab2_plane, offs2_sb)
        w2_codes = keep.tile([P, H], I32, name="w2_codes", align_bytes=64)
        nc.vector.tensor_copy(
            w2_codes[:].rearrange("p (g t m) -> p g m t", g=GROUPS, t=PACK),
            w2_sb[:].rearrange("p (g m t) -> p g m t", g=GROUPS, t=PACK),
        )
        v2_words = [gather_word_half("v2_words0", "v2_words0", tab2_sb, offs2_sb, 0)]
        w2_dealt = keep.tile([P, H], U8, name="w2_dealt", align_bytes=64)
        nc.vector.tensor_copy(
            w2_dealt[:].rearrange("p (g t m) -> p g t m", g=GROUPS, t=PACK),
            w2_plane[:].rearrange("p (g m t) -> p g t m", g=GROUPS, t=PACK),
        )
        v2_words.append(gather_word_half("v2_words1", "w2_plane", tab2_sb, offs2_sb, 1))
        v3_scales = gather_bytes("v3_scales", tab3_plane, offs3_sb)

        def pick_b(g):
            cols = slice(PASS * g, PASS * g + PASS)
            passes = [(w2_codes[:, cols], w2_dealt[:, cols], v2_words, v2_scales, V2_FIRST)]
            pairs = [
                keep.tile([P, 2, PICKS], F32, name="bp%d%d" % (g, u), tag="bp%d%d" % (g, u), align_bytes=64)
                for u in range(PACK // 2)
            ]
            for t in range(PACK):
                window = first_stage("b_rows", passes, t, None)
                nc.vector.tensor_copy(pairs[t // 2][:, t % 2, :], window[:].indirect(pos2_sb[:]))
            return pairs

        def pick_d(g):
            both = tables.tile([P, 2, PACK, PICKS], F32, name="picked%d" % g, tag="table%d" % g, align_bytes=64)
            passes = [w3_mx[g] + (v3_words, v3_scales, V3_FIRST)]
            for t in range(PACK):
                window = first_stage("d_rows", passes, t, bd_sb[:, g, t : t + 1])
                nc.vector.tensor_copy(both[:, 0, t, :], window[:].indirect(pos3_sb[:]))
            return both

        def pick_a_minus_b(g):
            passes = [w1_mx[g, a] + (v_words[a], v_scales, 4 * a) for a in range(K // PASS)]
            for t in range(PACK):
                window = first_stage("a_rows", passes, t, None)
                nc.vector.tensor_tensor(
                    picked[g][:, 1, t, :], window[:].indirect(pos1_sb[:]), bp[g][t // 2][:, t % 2, :], ALU.subtract
                )

        def damped_lamp(g, damp_slot, product_slot):
            damp = blocks.tile([P, PACK, PICKS], F32, name="damp%d" % g, tag="block" + damp_slot)
            parts = [damp[:, 2 * u : 2 * u + 2, :] for u in range(PACK // 2)]
            for part, source in zip(parts, bp[g]):
                nc.scalar.activation(part, source[:], ACT.Abs)
            for part in parts:
                nc.scalar.activation(part, part, ACT.Abs_reciprocal_sqrt, bias=1.0)
            for part in parts:
                nc.scalar.activation(part, part, ACT.Square)
            product = blocks.tile([P, PACK, PICKS], F32, name="lamp%d" % g, tag="block" + product_slot)
            nc.vector.tensor_tensor(product[:], damp[:], picked[g][:, 0], ALU.mult)
            return product

        def quantize_z(g, toks, z_bf, z_mx):
            nc.vector.tensor_tensor(
                woven_out(z_bf), woven_in(picked[g][:, 1, :, toks]), woven_in(lamp[g][:, :, toks]), ALU.mult
            )
            nc.vector.quantize_mx(out=z_mx[0][:, toks].bitcast(FP8X4), scales=z_mx[1][:, toks], in_=z_bf[:])

        bp = [pick_b(0)]
        v3_words = gather_words("v3_words", tab3_sb, offs3_sb)
        v_scales = gather_bytes("v_scales", tab_plane, offs_sb)
        w3_bf = keep.tile([P, PACK * BANK], BF16, name="w3_bf", tag="bp11", align_bytes=64)
        w3_mx = [quantize("w3_0", round_dealt(w3_bf, w3_blocks[0], on_scalar))]
        bp.append(pick_b(1))
        w3_mx.append(quantize("w3_1", round_dealt(rounded_tile("w3_bf", 0), w3_blocks[1], on_scalar)))

        w1_blocks = {(0, 0): load_w1(0, 0, "C")}
        tab_sb = [load_table("tab_sb", tab_words[0], 0)]
        w1_blocks[0, 1] = load_w1(0, 1, "D")
        tab_sb.append(load_table("tab_sb", tab_words[1], 1))
        w1_blocks[1, 1] = load_w1(1, 1, "B")
        w1_blocks[1, 0] = load_w1(1, 0, "A")
        pos1_sb = load_list("pos1_sb", pos1)
        w1_mx = {(0, 0): quantize("w1_00", round_dealt(rounded_tile("w1_bf", 1), w1_blocks[0, 0], on_vector))}
        v_words = [gather_words("v_words0", tab_sb[0], offs_sb)]
        picked = [pick_d(0)]
        w1_mx[0, 1] = quantize("w1_01", round_dealt(rounded_tile("w1_bf", 2), w1_blocks[0, 1], on_scalar))
        v_words.append(gather_words("v_words1", tab_sb[1], offs_sb))
        picked.append(pick_d(1))
        w1_mx[1, 1] = quantize("w1_11", round_dealt(rounded_tile("w1_bf", 0), w1_blocks[1, 1], on_vector))
        w1_mx[1, 0] = quantize("w1_10", round_dealt(rounded_tile("w1_bf", 3), w1_blocks[1, 0], on_scalar))

        w5_blocks = [load_block("w5_block", w5[PASS * g : PASS * g + PASS, :], "CE"[g]) for g in range(GROUPS)]
        w4_sb = keep.tile([P, GROUPS, 2 * N], U8, name="w4_sb", align_bytes=64)
        nc.sync.dma_start(w4_sb[:].bitcast(I32), w4_words.rearrange("a p n -> p a n").bitcast(I32))
        for q in range(QUADS):
            nc.sync.dma_start(
                w4_plane[32 * q : 32 * q + 4, :].rearrange("r (a n) -> r a n", a=GROUPS).bitcast(I32),
                w4_scales[:, 4 * q : 4 * q + 4, :].rearrange("a r n -> r a n").bitcast(I32),
            )
        bo_sb = lists.tile([P, N // P], F32, name="bo_sb")
        with nc.allow_non_contiguous_dma(reason="one bias value a partition"):
            nc.sync.dma_start(bo_sb[:], bo.rearrange("(c p) -> p c", p=P))
        w5_mx = {1: quantize("w5_1", round_woven(rounded_tile("w5_bf", 1), w5_blocks[1][:], on_scalar))}

        lamp = [damped_lamp(0, "D", "A")]
        pick_a_minus_b(0)
        z_mx = mx_tiles("z_0")
        quantize_z(0, slice(0, PICKS), rounded_tile("z_bf", 2), z_mx)
        lamp.append(damped_lamp(1, "B", "E"))
        pick_a_minus_b(1)

        final = {
            (h, u): psum.tile([P, 2, HALF], F32, name="final%d%d" % (h, u), tag="bank%d" % (BANKS - 4 + 2 * h + u))
            for h in range(2)
            for u in range(2)
        }

        def z_passes(g, h, z_mx):
            for c in range(N // P):
                for e in range(HALF // P):
                    toks = slice(HALF * h + P * e, HALF * h + P * e + P)
                    nc.tensor.matmul_mx(
                        out=final[h, c // 2][:, c % 2, P * e : P * e + P],
                        lhsT=w4_sb[:, g, 2 * P * c : 2 * P * c + 2 * P].bitcast(FP4X4),
                        lhsT_scale=w4_plane[:, N * g + P * c : N * g + P * c + P],
                        rhs=z_mx[0][:, toks].bitcast(FP8X4), rhs_scale=z_mx[1][:, toks],
                        start=(g == 0 and c % 2 == 0 and e == 0),
                        stop=(g == GROUPS - 1 and c % 2 == 1 and e == HALF // P - 1),
                    )

        def a_row_slot(t):
            return "rows%d" % ((2 * GROUPS * PACK + t) % ROW_SLOTS)

        for h in range(2):
            z_passes(0, h, z_mx)
        w5_mx[0] = quantize("w5_0", round_woven(rounded_tile("w5_bf", 3), w5_blocks[0][:], on_scalar))
        for g in range(GROUPS):
            dp_bf = rows.tile([P, PACK * PICKS], BF16, name="dp_bf", tag=a_row_slot(g), align_bytes=64)
            dp_codes, dp_scales = quantize("dp_%d" % g, round_woven(dp_bf, picked[g][:, 0], on_scalar))
            for h in range(2):
                toks = slice(HALF * h, HALF * h + HALF)
                for c in range(N // P):
                    cols = slice(P * c, P * c + P)
                    nc.tensor.matmul_mx(
                        out=final[h, c // 2][:, c % 2, :],
                        lhsT=w5_mx[g][0][:, cols].bitcast(FP8X4), lhsT_scale=w5_mx[g][1][:, cols],
                        rhs=dp_codes[:, toks].bitcast(FP8X4), rhs_scale=dp_scales[:, toks],
                        start=False, stop=False,
                    )

        z_mx = mx_tiles("z_1")
        for h in range(2):
            toks = slice(HALF * h, HALF * h + HALF)
            z_bf = rows.tile([P, PACK * HALF], BF16, name="z_bf", tag=a_row_slot(h), align_bytes=64)
            quantize_z(1, toks, z_bf, z_mx)
            z_passes(1, h, z_mx)
            for u in range(2):
                result = rows.tile([P, 2, HALF], F32, name="result", tag=next_slot("rows", ROW_SLOTS), align_bytes=64)
                for e in range(2):
                    bias = bo_sb[:, 2 * u + e : 2 * u + e + 1]
                    if (h, u) == (1, 1):
                        nc.vector.tensor_scalar(result[:, e, :], final[h, u][:, e, :], bias, None, ALU.add)
                    else:
                        nc.scalar.activation(result[:, e, :], final[h, u][:, e, :], ACT.Identity, bias=bias)
                nc.sync.dma_start(out[2 * P * u : 2 * P * u + 2 * P, toks].rearrange("(e p) n -> p e n", p=P), result[:])
